import numpy as np
import ml_dtypes


def mxq(x, axis, fmt="e4m3"):
    dtype, down = {"e4m3": (ml_dtypes.float8_e4m3fn, 7), "e5m2": (ml_dtypes.float8_e5m2, 14)}[fmt]
    v = np.moveaxis(np.asarray(x, np.float32).astype(ml_dtypes.bfloat16).astype(np.float64), axis, -1)
    blocks = v.reshape(v.shape[:-1] + (-1, 32))
    amax = np.abs(blocks).max(-1, keepdims=True)
    byte = np.maximum(np.where(amax > 0, np.frexp(amax)[1] - 1 + 127, 0) - down, 1)
    scale = np.exp2(byte - 127.0)
    codes = (blocks / scale).astype(np.float32).astype(dtype).astype(np.float64)
    return np.moveaxis((codes * scale).reshape(v.shape), -1, axis)


WIDE = False


def mx_kscale(k):
    if not WIDE:
        return np.ones(k)
    levels = np.array([10, -10, 5, -5, 0])
    if k % 512:
        return np.exp2(np.random.permutation(np.resize(levels, k // 32))).repeat(32)
    a = np.empty((k // 512, 16))
    for p in range(k // 512):
        a[p, :8] = np.random.permutation(np.resize(levels, 8))
        for g in range(8):
            far = levels[np.abs(levels - a[p, g]) >= 10]
            a[p, g + 8] = far[np.random.randint(len(far))]
    return np.exp2(a.ravel()).repeat(32)


def f64(x):
    return np.asarray(x).astype(np.float64)


def striped(idx):
    return np.tile(idx.reshape(-1, 16).T, (8, 1)).astype(np.uint16)


def unstriped(offs):
    return offs[:16].T.reshape(-1).astype(np.int64)


def striped8(idx):
    return np.concatenate([x.reshape(-1, 16).T for x in idx]).astype(np.uint16)


def runs(offs, k):
    lists = np.stack([offs[16 * r : 16 * r + 16].T.reshape(-1) for r in range(8)]).astype(np.int64)
    return lists[np.arange(k) % 512 // 64]


def pack_weight(w):
    k, n = w.shape
    w = f64(np.asarray(w, np.float32).astype(ml_dtypes.bfloat16)).reshape(k // 32, 32, n)
    amax = np.abs(w).max(1)
    byte = np.clip(np.where(amax > 0, np.frexp(amax)[1] - 1 + 127 - 7, 1), 1, 254)
    scaled = (w * np.exp2(127.0 - byte)[:, None, :]).reshape(k, n).astype(np.float32)
    words = np.ascontiguousarray(scaled.reshape(k // 512, 128, 4, n).transpose(0, 1, 3, 2)).astype(ml_dtypes.float8_e4m3fn).view(np.uint8)
    return words, np.ascontiguousarray(byte.astype(np.uint8).reshape(k // 512, 16, n))


def unpack_weight(words, scales):
    g, p, n, _ = words.shape
    vals = np.ascontiguousarray(words).view(ml_dtypes.float8_e4m3fn).astype(np.float64) * np.repeat(np.exp2(scales.astype(np.float64) - 127.0), 8, axis=1)[..., None]
    return vals.transpose(0, 1, 3, 2).reshape(g * 512, n)


E2M1 = np.array([0.0, 0.5, 1.0, 1.5, 2.0, 3.0, 4.0, 6.0, -0.0, -0.5, -1.0, -1.5, -2.0, -3.0, -4.0, -6.0])


def pack_fp4(w):
    k, n = w.shape
    w = f64(np.asarray(w, np.float32).astype(ml_dtypes.bfloat16)).reshape(k // 32, 32, n)
    amax = np.abs(w).max(1)
    mant, ex = np.frexp(amax / 6.0)
    byte = np.clip(np.where(amax > 0, np.where(mant > 0.5, ex, ex - 1) + 127, 1), 1, 254)
    scaled = (w * np.exp2(127.0 - byte)[:, None, :]).reshape(k, n).astype(np.float32)
    c = np.ascontiguousarray(scaled.reshape(k // 512, 128, 4, n).transpose(0, 1, 3, 2)).astype(ml_dtypes.float4_e2m1fn).view(np.uint8) & 0xF
    words = (c[..., 0::2] | (c[..., 1::2] << 4)).reshape(k // 512, 128, 2 * n)
    return np.ascontiguousarray(words), np.ascontiguousarray(byte.astype(np.uint8).reshape(k // 512, 16, n))


def unpack_fp4(words, scales):
    g, _, n = scales.shape
    words = np.ascontiguousarray(words).reshape(g, 128, n, 2)
    nib = np.empty((g, 128, n, 4), np.uint8)
    nib[..., 0::2] = words & 0xF
    nib[..., 1::2] = words >> 4
    vals = E2M1[nib] * np.repeat(np.exp2(scales.astype(np.float64) - 127.0), 8, axis=1)[..., None]
    return vals.transpose(0, 1, 3, 2).reshape(g * 512, n)


def sigmoid(v):
    return 1.0 / (1.0 + np.exp(-np.maximum(v, -700.0)))

def planes(y):
    n, m = y.shape
    v = y.astype(np.float32).astype(ml_dtypes.bfloat16).astype(np.float64).reshape(n // 32, 32, m)
    top = np.abs(v).max(1)
    byte = np.clip(np.where(top > 0, np.frexp(top)[1] - 1 + 127 - 7, 1), 1, 254)
    codes = (v * np.exp2(127.0 - byte)[:, None, :]).reshape(n, m).astype(np.float32).astype(ml_dtypes.float8_e4m3fn).view(np.uint8)
    words = codes.reshape(n // 512, 128, 4, m).transpose(0, 1, 3, 2)
    return np.ascontiguousarray(words), np.ascontiguousarray(byte.astype(np.uint8).reshape(n // 512, 16, m))


K, T, S, N, G, H, W = 512, 2048, 512, 512, 2048, 512, 256


def setup_inputs():
    n = np.random.standard_normal
    s = mx_kscale(K)[:, None]
    u = mx_kscale(S)
    packed_xT = pack_weight(n((K, T)) * s)
    packed_dT = pack_weight(n((K, G)) / s)
    packed_w1 = pack_fp4(n((H, N)) / np.sqrt(H) / u[:, None])
    perm = np.random.permutation(S)
    return {
        "x_words": packed_xT[0],
        "x_scales": packed_xT[1],
        "d_words": packed_dT[0],
        "d_scales": packed_dT[1],
        "gn": (np.random.uniform(0.5, 1.5, (H, 1)) * u[:, None]).astype(np.float32),
        "w1_words": packed_w1[0],
        "w1_scales": packed_w1[1],
        "offs": striped(np.random.permutation(T)[:S]),
        "k1": striped8(np.random.randint(0, G, (8, H))),
        "n1": striped(perm[:W]),
        "n2": striped(perm[W:]),
        "n3": striped(np.random.randint(0, S, G)),
    }


def reference(x_words, x_scales, d_words, d_scales, gn, w1_words, w1_scales, offs, k1, n1, n2, n3):
    d_k1 = unpack_weight(d_words, d_scales)[np.arange(K)[:, None], runs(k1, K)]
    xq = unpack_weight(x_words, x_scales)[:, unstriped(offs)]
    h = 0.0625 * (d_k1.T @ xq)
    pa = h[:, unstriped(n1)]
    pb = h[:, unstriped(n2)]
    ra = pa * sigmoid(pb)
    ds = h.copy()
    ds[:, unstriped(n2)] = ra
    z = f64(gn) * ds
    h2 = unpack_fp4(w1_words, w1_scales).T @ mxq(z, 0, "e4m3")
    mb = h2[:, unstriped(n3)]
    mx = mb.reshape(N, S, 4).max(axis=2)
    mn = mb.reshape(N, S, 4).min(axis=2)
    out_0 = mx * np.tanh(h2 - mn)
    return (out_0,) + planes(out_0)

@@ -1,0 +1,249 @@
+from contextlib import ExitStack
+
+import concourse.mybir as mybir
+
+K, T, S, N, G, H, W = 512, 2048, 512, 512, 2048, 512, 256
+FLOPS = 2 * K * H * S + 2 * H * N * S
+
+F32 = mybir.dt.float32
+BF16 = mybir.dt.bfloat16
+I32 = mybir.dt.int32
+U32 = mybir.dt.uint32
+U16 = mybir.dt.uint16
+U8 = mybir.dt.uint8
+FP8X4 = mybir.dt.float8_e4m3fn_x4
+FP4X4 = mybir.dt.float4_e2m1fn_x4
+ACT = mybir.ActivationFunctionType
+ALU = mybir.AluOpType
+
+P = 128
+PACK = 4
+MEMBERS = 4
+SPARE = 8
+GATHER = 512
+
+
+def tile_picked_pqlayfoldgtan_none_po_kernel(
+    tc, x_words, x_scales, d_words, d_scales, gn, w1_words, w1_scales, offs, k1, n1, n2, n3, out_0, out_1, out_2
+):
+    nc = tc.nc
+    with ExitStack() as ctx:
+        lists = ctx.enter_context(tc.tile_pool(name="lists", bufs=1))
+        keep = ctx.enter_context(tc.tile_pool(name="keep", bufs=1))
+        ring = ctx.enter_context(tc.tile_pool(name="ring", bufs=3))
+        psum = ctx.enter_context(tc.psum_pool(name="psum", bufs=1))
+
+        def held(name, shape, dtype):
+            return keep.tile(shape, dtype, name=name, align_bytes=64)
+
+        def load_list(name, src):
+            tile = lists.tile(list(src.shape), U16, name=name)
+            nc.sync.dma_start(tile[:], src)
+            return tile
+
+        def load_scale_rows(queue, name, scales):
+            width = scales.shape[2]
+            table = held(name, [P, width], U8)
+            rows = scales[0].bitcast(I32).unsqueeze(1).to_broadcast([16, 8, width // 4])
+            queue.dma_start(table[:].bitcast(I32), rows)
+            return table
+
+        k1_list = load_list("k1_list", k1)
+        d_scale_table = load_scale_rows(nc.sync, "d_scale_table", d_scales)
+        offs_list = load_list("offs_list", offs)
+        x_scale_table = load_scale_rows(nc.sync, "x_scale_table", x_scales)
+        d_table = held("d_table", [P, G], U32)
+        nc.sync.dma_start(d_table[:].bitcast(I32), d_words[0].rearrange("p n t -> p (n t)").bitcast(I32))
+        n2_list = load_list("n2_list", n2)
+        n1_list = load_list("n1_list", n1)
+        x_table = keep.tile([P, T], U32, name="x_table", tag="x_table", align_bytes=64)
+        nc.sync.dma_start(x_table[:].bitcast(I32), x_words[0].rearrange("p n t -> p (n t)").bitcast(I32))
+        n3_list = load_list("n3_list", n3)
+        w_raw = held("w_raw", [P, 2 * N], U8)
+        nc.gpsimd.dma_start(w_raw[:].bitcast(I32), w1_words[0].bitcast(I32))
+        w_scale_rows = load_scale_rows(nc.gpsimd, "w_scale_rows", w1_scales)
+        gain = held("gain", [P, PACK], F32)
+        nc.gpsimd.dma_start(gain[:], gn.rearrange("(p t) o -> p (t o)", t=PACK))
+
+        def gather_scale_rows(queue, plane):
+            for j in range(1, 4):
+                queue.dma_start(plane[j:P:32, :].bitcast(I32), plane[8 * j:P:32, :].bitcast(I32))
+
+        d_scale_picked = held("d_scale_picked", [P, H], U8)
+        nc.vector.tensor_copy(d_scale_picked[:], d_scale_table[:].indirect(k1_list[:]))
+        d_plane = held("d_plane", [P, H], U8)
+        nc.vector.tensor_copy(
+            d_plane[:].rearrange("p (t m) -> p t m", t=PACK),
+            d_scale_picked[:].rearrange("p (m t) -> p t m", t=PACK),
+        )
+        gather_scale_rows(nc.scalar, d_plane)
+        x_scale_picked = held("x_scale_picked", [P, S], U8)
+        nc.vector.tensor_copy(x_scale_picked[:], x_scale_table[:].indirect(offs_list[:]))
+        x_plane = held("x_plane", [P, S], U8)
+        nc.vector.tensor_copy(x_plane[:].bitcast(I32), x_scale_picked[:].bitcast(I32))
+        gather_scale_rows(nc.scalar, x_plane)
+        d_picked = held("d_picked", [P, H], U32)
+        nc.vector.tensor_copy(d_picked[:], d_table[:].indirect(k1_list[:]))
+        d_codes = held("d_codes", [P, H], U32)
+        nc.vector.tensor_copy(
+            d_codes[:].rearrange("p (t m) -> p m t", t=PACK),
+            d_picked[:].rearrange("p (m t) -> p m t", t=PACK),
+        )
+        x_codes = held("x_codes", [P, S], U32)
+        half = S // 2
+        for u in range(2):
+            nc.vector.tensor_copy(
+                x_codes[:, u * half:(u + 1) * half],
+                x_table[:].indirect(offs_list[:, u * half // 16:(u + 1) * half // 16]),
+            )
+
+        w_plane = keep.tile([P, N], U8, name="w_plane", tag="x_table", align_bytes=64)
+        nc.vector.tensor_copy(
+            w_plane[:].rearrange("p (t m) -> p t m", t=PACK),
+            w_scale_rows[:].rearrange("p (m t) -> p t m", t=PACK),
+        )
+        gather_scale_rows(nc.sync, w_plane)
+
+        z_pairs = held("z_pairs", [P, 2, S, 2], BF16)
+        h_acc = [psum.tile([P, S], F32, name="h_acc%d" % t) for t in range(PACK)]
+        pass_order = [(t, u) for pair in range(2) for u in range(2) for t in (2 * pair, 2 * pair + 1)]
+        for t, u in pass_order:
+            tokens = slice(u * half, (u + 1) * half)
+            cols = slice(t * P, (t + 1) * P)
+            nc.tensor.matmul_mx(
+                out=h_acc[t][:, tokens], lhsT=d_codes[:, cols].bitcast(FP8X4), lhsT_scale=d_plane[:, cols],
+                rhs=x_codes[:, tokens].bitcast(FP8X4), rhs_scale=x_plane[:, tokens], start=True, stop=True,
+            )
+        h_rows = [held("h%d" % t, [P, S], F32) for t in range(PACK)]
+        for t in range(PACK):
+            nc.vector.tensor_scalar(h_rows[t][:], h_acc[t][:], 0.0625, None, ALU.mult)
+        gate = [held("gate%d" % t, [P, W], F32) for t in range(PACK)]
+        fetched = [keep.tile([P, W], F32, name="fetched%d" % t, tag="fetched%d" % t, align_bytes=64) for t in range(PACK)]
+
+        def fetch_gate(t):
+            nc.scalar.activation(gate[t][:], h_rows[t][:].indirect(n2_list[:]), ACT.Sigmoid)
+
+        def fetch_partner(t):
+            nc.scalar.activation(fetched[t][:], h_rows[t][:].indirect(n1_list[:]), ACT.Copy)
+
+        fetch_gate(0)
+        fetch_gate(1)
+        fetch_partner(0)
+        fetch_gate(2)
+        fetch_gate(3)
+        fetch_partner(3)
+        for by_scalar, by_vector in ((1, 0), (2, 3)):
+            t = by_scalar
+            nc.vector.tensor_tensor(fetched[t][:], h_rows[t][:].indirect(n1_list[:]), gate[t][:], ALU.mult)
+            nc.scalar.activation(h_rows[t][:].indirect(n2_list[:]), fetched[t][:], ACT.Copy)
+            t = by_vector
+            nc.vector.tensor_tensor(h_rows[t][:].indirect(n2_list[:]), fetched[t][:], gate[t][:], ALU.mult)
+        for t in (0, 3, 1, 2):
+            nc.vector.tensor_scalar(z_pairs[:, t // 2, :, t % 2], h_rows[t][:], gain[:, t:t + 1], None, ALU.mult)
+        w_codes = keep.tile([P, 2 * N], U8, name="w_codes", tag="fetched2", align_bytes=64)
+        nc.scalar.copy(
+            w_codes[:].bitcast(U16).rearrange("p (t m) -> p t m", t=PACK),
+            w_raw[:].bitcast(U16).rearrange("p (m t) -> p t m", t=PACK),
+        )
+
+        z_codes = held("z_codes", [P, S], U32)
+        z_plane = held("z_plane", [P, S], U8)
+        z_words = z_pairs[:].rearrange("p a j e -> p a (j e)").bitcast(I32)
+        h2_acc = [psum.tile([P, S], F32, name="h2_acc%d" % t) for t in range(PACK)]
+        z_grouped = [held("z_grouped%d" % u, [P, half * PACK], BF16) for u in range(2)]
+        for u in range(2):
+            cols = slice(u * half, (u + 1) * half)
+            nc.vector.tensor_copy(
+                z_grouped[u][:].bitcast(I32).rearrange("p (j a) -> p j a", a=2),
+                z_words[:, :, cols].rearrange("p a j -> p j a"),
+            )
+        for u in range(2):
+            cols = slice(u * half, (u + 1) * half)
+            nc.vector.quantize_mx(out=z_codes[:, cols].bitcast(FP8X4), scales=z_plane[:, cols], in_=z_grouped[u][:])
+        for t, u in pass_order:
+            cols = slice(u * half, (u + 1) * half)
+            nc.tensor.matmul_mx(
+                out=h2_acc[t][:, cols],
+                lhsT=w_codes[:, 2 * t * P:2 * (t + 1) * P].bitcast(FP4X4),
+                lhsT_scale=w_plane[:, t * P:(t + 1) * P],
+                rhs=z_codes[:, cols].bitcast(FP8X4), rhs_scale=z_plane[:, cols], start=True, stop=True,
+            )
+        h2_rows = []
+        for t in range(PACK):
+            h2 = held("h2_%d" % t, [P, S + SPARE], F32)
+            nc.gpsimd.memset(h2[:, S:], 0.0)
+            if t == 1:
+                nc.vector.tensor_copy(h2[:, :S], h2_acc[t][:])
+            else:
+                nc.scalar.copy(h2[:, :S], h2_acc[t][:])
+            h2_rows.append(h2)
+
+        out_rows = out_0.rearrange("(p t) j -> p t j", t=PACK)
+        out_words = out_1[0].rearrange("p n t -> p (n t)").bitcast(I32)
+        result = [held("result%d" % u, [P, PACK, half], F32) for u in range(2)]
+        out_plane = [held("out_plane%d" % u, [P, half], U8) for u in range(2)]
+
+        def members(t, lo, hi, on_vector):
+            width = hi - lo
+            mb = ring.tile([P, half * MEMBERS], F32, name="mb")
+            for e in range(lo * MEMBERS, hi * MEMBERS, GATHER):
+                window = h2_rows[t][:].indirect(n3_list[:, e // 16:(e + GATHER) // 16])
+                dst = mb[:, e - lo * MEMBERS:e - lo * MEMBERS + GATHER]
+                if on_vector:
+                    nc.vector.tensor_copy(dst, window)
+                else:
+                    nc.scalar.activation(dst, window, ACT.Copy)
+            quads = mb[:, :width * MEMBERS].rearrange("p (j a e) -> p j a e", a=2, e=2)
+            low2 = ring.tile([P, half, 2], F32, name="low2")
+            high2 = ring.tile([P, half, 2], F32, name="high2")
+            nc.vector.tensor_tensor(low2[:, :width, :], quads[:, :, 0, :], quads[:, :, 1, :], ALU.min)
+            nc.vector.tensor_tensor(high2[:, :width, :], quads[:, :, 0, :], quads[:, :, 1, :], ALU.max)
+            low = ring.tile([P, half], F32, name="low")
+            high = ring.tile([P, half], F32, name="high")
+            nc.vector.tensor_tensor(low[:, :width], low2[:, :width, 0], low2[:, :width, 1], ALU.min)
+            nc.vector.tensor_tensor(high[:, :width], high2[:, :width, 0], high2[:, :width, 1], ALU.max)
+            rise = mb[:, :width]
+            nc.vector.tensor_tensor(rise, h2_rows[t][:, lo:hi], low[:, :width], ALU.subtract)
+            squashed = ring.tile([P, half], F32, name="squashed")
+            nc.scalar.activation(squashed[:, :width], rise, ACT.Tanh)
+            return high, squashed
+
+        def finish(t, lo, hi, high, squashed):
+            width = hi - lo
+            u, at = lo // half, lo % half
+            nc.vector.tensor_tensor(result[u][:, t, at:at + width], high[:, :width], squashed[:, :width], ALU.mult)
+            nc.sync.dma_start(out_rows[:, t, lo:hi], result[u][:, t, at:at + width])
+            if t == PACK - 1:
+                planes(lo, hi)
+                if hi % half == 0:
+                    store_scales(u)
+
+        def planes(lo, hi):
+            width = hi - lo
+            u, at = lo // half, lo % half
+            grouped = held("out_grouped%d" % lo, [P, width * PACK], BF16)
+            nc.vector.tensor_copy(
+                grouped[:].rearrange("p (c i t) -> p c t i", i=4, t=PACK),
+                result[u][:, :, at:at + width].rearrange("p t (c i) -> p c t i", i=4),
+            )
+            codes = held("out_codes%d" % lo, [P, width], U32)
+            nc.vector.quantize_mx(out=codes[:].bitcast(FP8X4), scales=out_plane[u][:, at:at + width], in_=grouped[:])
+            nc.sync.dma_start(out_words[:, lo:hi], codes[:].bitcast(I32))
+
+        def store_scales(u):
+            for j in range(4):
+                queue = nc.sync if j % 2 == 0 else nc.scalar
+                queue.dma_start(
+                    out_2[0, j:16:4, u * half:(u + 1) * half].bitcast(I32), out_plane[u][j:P:32, :].bitcast(I32)
+                )
+
+        quarter = half // 2
+        units = [(t, 0, half) for t in (1, 0, 2, 3)] + [(t, half, S) for t in range(PACK - 1)]
+        units = units + [(PACK - 1, lo, lo + quarter) for lo in (half, half + quarter)]
+        pending = None
+        for n, (t, lo, hi) in enumerate(units):
+            made = members(t, lo, hi, n == 0)
+            if pending is not None:
+                finish(*pending)
+            pending = (t, lo, hi) + made
+        finish(*pending)

@@ -41,29 +41,30 @@ def tile_picked_pqlayfoldgtan_none_po_kernel(
             nc.sync.dma_start(tile[:], src)
             return tile
 
-        def load_scale_rows(queue, name, scales):
+        def shared(name, shape, dtype, tag):
+            return keep.tile(shape, dtype, name=name, tag=tag, align_bytes=64)
+
+        def load_scale_rows(queue, table, scales):
             width = scales.shape[2]
-            table = held(name, [P, width], U8)
             rows = scales[0].bitcast(I32).unsqueeze(1).to_broadcast([16, 8, width // 4])
             queue.dma_start(table[:].bitcast(I32), rows)
-            return table
 
         k1_list = load_list("k1_list", k1)
-        d_scale_table = load_scale_rows(nc.sync, "d_scale_table", d_scales)
+        d_scale_table = held("d_scale_table", [P, G], U8)
+        load_scale_rows(nc.sync, d_scale_table, d_scales)
         offs_list = load_list("offs_list", offs)
-        x_scale_table = load_scale_rows(nc.sync, "x_scale_table", x_scales)
-        d_table = held("d_table", [P, G], U32)
-        nc.sync.dma_start(d_table[:].bitcast(I32), d_words[0].rearrange("p n t -> p (n t)").bitcast(I32))
+        x_scale_table = held("x_scale_table", [P, T], U8)
+        load_scale_rows(nc.sync, x_scale_table, x_scales)
         n2_list = load_list("n2_list", n2)
         n1_list = load_list("n1_list", n1)
-        x_table = keep.tile([P, T], U32, name="x_table", tag="x_table", align_bytes=64)
-        nc.sync.dma_start(x_table[:].bitcast(I32), x_words[0].rearrange("p n t -> p (n t)").bitcast(I32))
         n3_list = load_list("n3_list", n3)
-        w_raw = held("w_raw", [P, 2 * N], U8)
-        nc.gpsimd.dma_start(w_raw[:].bitcast(I32), w1_words[0].bitcast(I32))
-        w_scale_rows = load_scale_rows(nc.gpsimd, "w_scale_rows", w1_scales)
-        gain = held("gain", [P, PACK], F32)
-        nc.gpsimd.dma_start(gain[:], gn.rearrange("(p t) o -> p (t o)", t=PACK))
+        d_table = shared("d_table", [P, G], U32, "d_table")
+        nc.sync.dma_start(d_table[:].bitcast(I32), d_words[0].rearrange("p n t -> p (n t)").bitcast(I32))
+        x_table = shared("x_table", [P, T], U32, "x_table")
+        nc.sync.dma_start(x_table[:].bitcast(I32), x_words[0].rearrange("p n t -> p (n t)").bitcast(I32))
+        h2_rows = [held("h2_%d" % t, [P, S + SPARE], F32) for t in range(PACK)]
+        for t in range(PACK):
+            nc.gpsimd.memset(h2_rows[t][:, S:], 0.0)
 
         def gather_scale_rows(queue, plane):
             for j in range(1, 4):
@@ -77,18 +78,24 @@ def tile_picked_pqlayfoldgtan_none_po_kernel(
             d_scale_picked[:].rearrange("p (m t) -> p t m", t=PACK),
         )
         gather_scale_rows(nc.scalar, d_plane)
-        x_scale_picked = held("x_scale_picked", [P, S], U8)
+        x_scale_picked = shared("x_scale_picked", [P, S], U8, "x_scale_picked")
         nc.vector.tensor_copy(x_scale_picked[:], x_scale_table[:].indirect(offs_list[:]))
         x_plane = held("x_plane", [P, S], U8)
         nc.vector.tensor_copy(x_plane[:].bitcast(I32), x_scale_picked[:].bitcast(I32))
         gather_scale_rows(nc.scalar, x_plane)
-        d_picked = held("d_picked", [P, H], U32)
+        w_scale_rows = shared("w_scale_rows", [P, N], U8, "x_scale_picked")
+        load_scale_rows(nc.scalar, w_scale_rows, w1_scales)
+        d_picked = shared("d_picked", [P, H], U32, "d_picked")
         nc.vector.tensor_copy(d_picked[:], d_table[:].indirect(k1_list[:]))
+        w_raw = shared("w_raw", [P, 2 * N], U8, "d_table")
+        nc.sync.dma_start(w_raw[:].bitcast(I32), w1_words[0].bitcast(I32))
         d_codes = held("d_codes", [P, H], U32)
         nc.vector.tensor_copy(
             d_codes[:].rearrange("p (t m) -> p m t", t=PACK),
             d_picked[:].rearrange("p (m t) -> p m t", t=PACK),
         )
+        gain = shared("gain", [P, PACK], F32, "d_picked")
+        nc.sync.dma_start(gain[:], gn.rearrange("(p t) o -> p (t o)", t=PACK))
         x_codes = held("x_codes", [P, S], U32)
         half = S // 2
         for u in range(2):
@@ -132,14 +139,18 @@ def tile_picked_pqlayfoldgtan_none_po_kernel(
         fetch_gate(2)
         fetch_gate(3)
         fetch_partner(3)
-        for by_scalar, by_vector in ((1, 0), (2, 3)):
-            t = by_scalar
-            nc.vector.tensor_tensor(fetched[t][:], h_rows[t][:].indirect(n1_list[:]), gate[t][:], ALU.mult)
-            nc.scalar.activation(h_rows[t][:].indirect(n2_list[:]), fetched[t][:], ACT.Copy)
-            t = by_vector
-            nc.vector.tensor_tensor(h_rows[t][:].indirect(n2_list[:]), fetched[t][:], gate[t][:], ALU.mult)
-        for t in (0, 3, 1, 2):
-            nc.vector.tensor_scalar(z_pairs[:, t // 2, :, t % 2], h_rows[t][:], gain[:, t:t + 1], None, ALU.mult)
+        for t in (1, 0, 2, 3):
+            if t in (0, PACK - 1):
+                nc.vector.tensor_tensor(h_rows[t][:].indirect(n2_list[:]), fetched[t][:], gate[t][:], ALU.mult)
+            else:
+                nc.vector.tensor_tensor(fetched[t][:], h_rows[t][:].indirect(n1_list[:]), gate[t][:], ALU.mult)
+                nc.scalar.activation(h_rows[t][:].indirect(n2_list[:]), fetched[t][:], ACT.Copy)
+
+        def round_gained(t, cols):
+            nc.vector.tensor_scalar(z_pairs[:, t // 2, cols, t % 2], h_rows[t][:, cols], gain[:, t:t + 1], None, ALU.mult)
+
+        for t in (0, 3, 1):
+            round_gained(t, slice(0, S))
         w_codes = keep.tile([P, 2 * N], U8, name="w_codes", tag="fetched2", align_bytes=64)
         nc.scalar.copy(
             w_codes[:].bitcast(U16).rearrange("p (t m) -> p t m", t=PACK),
@@ -153,6 +164,7 @@ def tile_picked_pqlayfoldgtan_none_po_kernel(
         z_grouped = [held("z_grouped%d" % u, [P, half * PACK], BF16) for u in range(2)]
         for u in range(2):
             cols = slice(u * half, (u + 1) * half)
+            round_gained(2, cols)
             nc.vector.tensor_copy(
                 z_grouped[u][:].bitcast(I32).rearrange("p (j a) -> p j a", a=2),
                 z_words[:, :, cols].rearrange("p a j -> p j a"),
@@ -168,61 +180,70 @@ def tile_picked_pqlayfoldgtan_none_po_kernel(
                 lhsT_scale=w_plane[:, t * P:(t + 1) * P],
                 rhs=z_codes[:, cols].bitcast(FP8X4), rhs_scale=z_plane[:, cols], start=True, stop=True,
             )
-        h2_rows = []
         for t in range(PACK):
-            h2 = held("h2_%d" % t, [P, S + SPARE], F32)
-            nc.gpsimd.memset(h2[:, S:], 0.0)
-            if t == 1:
-                nc.vector.tensor_copy(h2[:, :S], h2_acc[t][:])
+            if t % 2 == 1:
+                nc.vector.tensor_copy(h2_rows[t][:, :S], h2_acc[t][:])
             else:
-                nc.scalar.copy(h2[:, :S], h2_acc[t][:])
-            h2_rows.append(h2)
+                nc.scalar.copy(h2_rows[t][:, :S], h2_acc[t][:])
 
         out_rows = out_0.rearrange("(p t) j -> p t j", t=PACK)
         out_words = out_1[0].rearrange("p n t -> p (n t)").bitcast(I32)
         result = [held("result%d" % u, [P, PACK, half], F32) for u in range(2)]
         out_plane = [held("out_plane%d" % u, [P, half], U8) for u in range(2)]
 
-        def members(t, lo, hi, on_vector):
+        def members(pair, lo, hi, first):
             width = hi - lo
-            mb = ring.tile([P, half * MEMBERS], F32, name="mb")
-            for e in range(lo * MEMBERS, hi * MEMBERS, GATHER):
-                window = h2_rows[t][:].indirect(n3_list[:, e // 16:(e + GATHER) // 16])
-                dst = mb[:, e - lo * MEMBERS:e - lo * MEMBERS + GATHER]
-                if on_vector:
-                    nc.vector.tensor_copy(dst, window)
-                else:
-                    nc.scalar.activation(dst, window, ACT.Copy)
-            quads = mb[:, :width * MEMBERS].rearrange("p (j a e) -> p j a e", a=2, e=2)
-            low2 = ring.tile([P, half, 2], F32, name="low2")
-            high2 = ring.tile([P, half, 2], F32, name="high2")
-            nc.vector.tensor_tensor(low2[:, :width, :], quads[:, :, 0, :], quads[:, :, 1, :], ALU.min)
-            nc.vector.tensor_tensor(high2[:, :width, :], quads[:, :, 0, :], quads[:, :, 1, :], ALU.max)
-            low = ring.tile([P, half], F32, name="low")
-            high = ring.tile([P, half], F32, name="high")
-            nc.vector.tensor_tensor(low[:, :width], low2[:, :width, 0], low2[:, :width, 1], ALU.min)
-            nc.vector.tensor_tensor(high[:, :width], high2[:, :width, 0], high2[:, :width, 1], ALU.max)
-            rise = mb[:, :width]
-            nc.vector.tensor_tensor(rise, h2_rows[t][:, lo:hi], low[:, :width], ALU.subtract)
-            squashed = ring.tile([P, half], F32, name="squashed")
-            nc.scalar.activation(squashed[:, :width], rise, ACT.Tanh)
-            return high, squashed
+            entries = width * MEMBERS
+            mb = ring.tile([P, 2 * half * MEMBERS], F32, name="mb")
+            for r in range(2):
+                for e in range(0, entries, GATHER):
+                    at = lo * MEMBERS + e
+                    window = h2_rows[2 * pair + r][:].indirect(n3_list[:, at // 16:(at + GATHER) // 16])
+                    dst = mb[:, r * entries + e:r * entries + e + GATHER]
+                    if first and r == 1:
+                        nc.vector.tensor_copy(dst, window)
+                    else:
+                        nc.scalar.activation(dst, window, ACT.Copy)
+            quads = mb[:, :2 * entries].rearrange("p (j a e) -> p j a e", a=2, e=2)
+            low2 = ring.tile([P, 2 * half, 2], F32, name="low2")
+            high2 = ring.tile([P, 2 * half, 2], F32, name="high2")
+            step = width if width == half and not first else 2 * width
+            for at in range(0, 2 * width, step):
+                part = slice(at, at + step)
+                nc.vector.tensor_tensor(low2[:, part, :], quads[:, part, 0, :], quads[:, part, 1, :], ALU.min)
+                nc.vector.tensor_tensor(high2[:, part, :], quads[:, part, 0, :], quads[:, part, 1, :], ALU.max)
+            both = slice(0, 2 * width)
+            low = ring.tile([P, 2 * half], F32, name="low")
+            high = ring.tile([P, 2 * half], F32, name="high")
+            nc.vector.tensor_tensor(low[:, both], low2[:, both, 0], low2[:, both, 1], ALU.min)
+            nc.vector.tensor_tensor(high[:, both], high2[:, both, 0], high2[:, both, 1], ALU.max)
+            for r in range(2):
+                part = slice(r * width, (r + 1) * width)
+                nc.vector.tensor_tensor(mb[:, part], h2_rows[2 * pair + r][:, lo:hi], low[:, part], ALU.subtract)
+            squashed = ring.tile([P, 2 * half], F32, name="squashed")
+            nc.scalar.activation(squashed[:, both], mb[:, both], ACT.Tanh)
+            return high[:, both], squashed[:, both]
 
-        def finish(t, lo, hi, high, squashed):
+        def finish(pair, lo, hi, high, squashed, last):
             width = hi - lo
             u, at = lo // half, lo % half
-            nc.vector.tensor_tensor(result[u][:, t, at:at + width], high[:, :width], squashed[:, :width], ALU.mult)
-            nc.sync.dma_start(out_rows[:, t, lo:hi], result[u][:, t, at:at + width])
-            if t == PACK - 1:
-                planes(lo, hi)
+            rows = slice(2 * pair, 2 * pair + 2)
+            nc.vector.tensor_tensor(
+                result[u][:, rows, at:at + width], high.rearrange("p (r j) -> p r j", r=2),
+                squashed.rearrange("p (r j) -> p r j", r=2), ALU.mult,
+            )
+            nc.sync.dma_start(out_rows[:, rows, lo:hi], result[u][:, rows, at:at + width])
+            if pair == 1:
+                planes(lo, hi, last)
                 if hi % half == 0:
                     store_scales(u)
 
-        def planes(lo, hi):
+        def planes(lo, hi, last):
             width = hi - lo
             u, at = lo // half, lo % half
             grouped = held("out_grouped%d" % lo, [P, width * PACK], BF16)
-            nc.vector.tensor_copy(
+            round_copy = nc.vector.tensor_copy if last else nc.scalar.copy
+            round_copy(
                 grouped[:].rearrange("p (c i t) -> p c t i", i=4, t=PACK),
                 result[u][:, :, at:at + width].rearrange("p t (c i) -> p c t i", i=4),
             )
@@ -238,12 +259,11 @@ def tile_picked_pqlayfoldgtan_none_po_kernel(
                 )
 
         quarter = half // 2
-        units = [(t, 0, half) for t in (1, 0, 2, 3)] + [(t, half, S) for t in range(PACK - 1)]
-        units = units + [(PACK - 1, lo, lo + quarter) for lo in (half, half + quarter)]
-        pending = None
-        for n, (t, lo, hi) in enumerate(units):
-            made = members(t, lo, hi, n == 0)
-            if pending is not None:
-                finish(*pending)
-            pending = (t, lo, hi) + made
-        finish(*pending)
+        units = [(0, 0, half), (1, 0, half), (0, half, S), (1, half, half + quarter), (1, half + quarter, S)]
+        lag = 2
+        made = []
+        for n in range(len(units) + lag):
+            if n < len(units):
+                made.append(members(*units[n], n == 0))
+            if n >= lag:
+                finish(*units[n - lag], *made[n - lag], n - lag == len(units) - 1)

@@ -49,15 +49,16 @@ def tile_picked_pqlayfoldgtan_none_po_kernel(
             rows = scales[0].bitcast(I32).unsqueeze(1).to_broadcast([16, 8, width // 4])
             queue.dma_start(table[:].bitcast(I32), rows)
 
-        k1_list = load_list("k1_list", k1)
         d_scale_table = held("d_scale_table", [P, G], U8)
+        x_scale_table = held("x_scale_table", [P, T], U8)
+        nc.vector.memset(x_scale_table[:].bitcast(I32), 0)
+        k1_list = load_list("k1_list", k1)
         load_scale_rows(nc.sync, d_scale_table, d_scales)
         offs_list = load_list("offs_list", offs)
-        x_scale_table = held("x_scale_table", [P, T], U8)
-        load_scale_rows(nc.sync, x_scale_table, x_scales)
         n2_list = load_list("n2_list", n2)
         n1_list = load_list("n1_list", n1)
         n3_list = load_list("n3_list", n3)
+        nc.sync.dma_start(x_scale_table[0:P:8, :].bitcast(I32), x_scales[0].bitcast(I32))
         d_table = shared("d_table", [P, G], U32, "d_table")
         nc.sync.dma_start(d_table[:].bitcast(I32), d_words[0].rearrange("p n t -> p (n t)").bitcast(I32))
         x_table = shared("x_table", [P, T], U32, "x_table")
@@ -112,18 +113,35 @@ def tile_picked_pqlayfoldgtan_none_po_kernel(
         gather_scale_rows(nc.sync, w_plane)
 
         z_pairs = held("z_pairs", [P, 2, S, 2], BF16)
-        h_acc = [psum.tile([P, S], F32, name="h_acc%d" % t) for t in range(PACK)]
+
+        def accumulators(name):
+            acc = []
+            for t in range(PACK):
+                if t < 2:
+                    acc.append([psum.tile([P, half], F32, name="%s%d_%d" % (name, t, u), tag="bank%d_%d" % (t, u))[:] for u in range(2)])
+                else:
+                    bank = psum.tile([P, S], F32, name="%s%d" % (name, t), tag="bank%d" % t)
+                    acc.append([bank[:, :half], bank[:, half:], bank[:]])
+            return acc
+
+        def pieces(acc, t):
+            if t < 2:
+                return [(slice(u * half, (u + 1) * half), acc[t][u]) for u in range(2)]
+            return [(slice(0, S), acc[t][2])]
+
+        h_acc = accumulators("h_acc")
         pass_order = [(t, u) for pair in range(2) for u in range(2) for t in (2 * pair, 2 * pair + 1)]
         for t, u in pass_order:
             tokens = slice(u * half, (u + 1) * half)
             cols = slice(t * P, (t + 1) * P)
             nc.tensor.matmul_mx(
-                out=h_acc[t][:, tokens], lhsT=d_codes[:, cols].bitcast(FP8X4), lhsT_scale=d_plane[:, cols],
+                out=h_acc[t][u], lhsT=d_codes[:, cols].bitcast(FP8X4), lhsT_scale=d_plane[:, cols],
                 rhs=x_codes[:, tokens].bitcast(FP8X4), rhs_scale=x_plane[:, tokens], start=True, stop=True,
             )
         h_rows = [held("h%d" % t, [P, S], F32) for t in range(PACK)]
         for t in range(PACK):
-            nc.vector.tensor_scalar(h_rows[t][:], h_acc[t][:], 0.0625, None, ALU.mult)
+            for cols, acc in pieces(h_acc, t):
+                nc.vector.tensor_scalar(h_rows[t][:, cols], acc, 0.0625, None, ALU.mult)
         gate = [held("gate%d" % t, [P, W], F32) for t in range(PACK)]
         fetched = [keep.tile([P, W], F32, name="fetched%d" % t, tag="fetched%d" % t, align_bytes=64) for t in range(PACK)]
 
@@ -160,7 +178,7 @@ def tile_picked_pqlayfoldgtan_none_po_kernel(
         z_codes = held("z_codes", [P, S], U32)
         z_plane = held("z_plane", [P, S], U8)
         z_words = z_pairs[:].rearrange("p a j e -> p a (j e)").bitcast(I32)
-        h2_acc = [psum.tile([P, S], F32, name="h2_acc%d" % t) for t in range(PACK)]
+        h2_acc = accumulators("h2_acc")
         z_grouped = [held("z_grouped%d" % u, [P, half * PACK], BF16) for u in range(2)]
         for u in range(2):
             cols = slice(u * half, (u + 1) * half)
@@ -175,95 +193,82 @@ def tile_picked_pqlayfoldgtan_none_po_kernel(
         for t, u in pass_order:
             cols = slice(u * half, (u + 1) * half)
             nc.tensor.matmul_mx(
-                out=h2_acc[t][:, cols],
+                out=h2_acc[t][u],
                 lhsT=w_codes[:, 2 * t * P:2 * (t + 1) * P].bitcast(FP4X4),
                 lhsT_scale=w_plane[:, t * P:(t + 1) * P],
                 rhs=z_codes[:, cols].bitcast(FP8X4), rhs_scale=z_plane[:, cols], start=True, stop=True,
             )
         for t in range(PACK):
-            if t % 2 == 1:
-                nc.vector.tensor_copy(h2_rows[t][:, :S], h2_acc[t][:])
-            else:
-                nc.scalar.copy(h2_rows[t][:, :S], h2_acc[t][:])
+            empty = nc.vector.tensor_copy if t % 2 == 1 else nc.scalar.copy
+            for cols, acc in pieces(h2_acc, t):
+                empty(h2_rows[t][:, cols], acc)
 
         out_rows = out_0.rearrange("(p t) j -> p t j", t=PACK)
         out_words = out_1[0].rearrange("p n t -> p (n t)").bitcast(I32)
-        result = [held("result%d" % u, [P, PACK, half], F32) for u in range(2)]
-        out_plane = [held("out_plane%d" % u, [P, half], U8) for u in range(2)]
+        result = held("result", [P, PACK, S], F32)
 
-        def members(pair, lo, hi, first):
+        def members(tiles, lo, hi, on_vector):
             width = hi - lo
-            entries = width * MEMBERS
-            mb = ring.tile([P, 2 * half * MEMBERS], F32, name="mb")
-            for r in range(2):
-                for e in range(0, entries, GATHER):
-                    at = lo * MEMBERS + e
-                    window = h2_rows[2 * pair + r][:].indirect(n3_list[:, at // 16:(at + GATHER) // 16])
-                    dst = mb[:, r * entries + e:r * entries + e + GATHER]
-                    if first and r == 1:
-                        nc.vector.tensor_copy(dst, window)
-                    else:
-                        nc.scalar.activation(dst, window, ACT.Copy)
-            quads = mb[:, :2 * entries].rearrange("p (j a e) -> p j a e", a=2, e=2)
-            low2 = ring.tile([P, 2 * half, 2], F32, name="low2")
-            high2 = ring.tile([P, 2 * half, 2], F32, name="high2")
-            step = width if width == half and not first else 2 * width
-            for at in range(0, 2 * width, step):
+            count = len(tiles) * width
+            mb = ring.tile([P, S * MEMBERS], F32, name="mb")
+            looks = [(t, e) for t in tiles for e in range(lo * MEMBERS, hi * MEMBERS, GATHER)]
+            for n, (t, e) in enumerate(looks):
+                window = h2_rows[t][:].indirect(n3_list[:, e // 16:(e + GATHER) // 16])
+                dst = mb[:, n * GATHER:(n + 1) * GATHER]
+                if n >= len(looks) - on_vector:
+                    nc.vector.tensor_copy(dst, window)
+                else:
+                    nc.scalar.activation(dst, window, ACT.Copy)
+            quads = mb[:, :count * MEMBERS].rearrange("p (j a e) -> p j a e", a=2, e=2)
+            low2 = ring.tile([P, S, 2], F32, name="low2")
+            high2 = ring.tile([P, S, 2], F32, name="high2")
+            step = count if on_vector == 2 else half
+            for at in range(0, count, step):
                 part = slice(at, at + step)
                 nc.vector.tensor_tensor(low2[:, part, :], quads[:, part, 0, :], quads[:, part, 1, :], ALU.min)
                 nc.vector.tensor_tensor(high2[:, part, :], quads[:, part, 0, :], quads[:, part, 1, :], ALU.max)
-            both = slice(0, 2 * width)
-            low = ring.tile([P, 2 * half], F32, name="low")
-            high = ring.tile([P, 2 * half], F32, name="high")
-            nc.vector.tensor_tensor(low[:, both], low2[:, both, 0], low2[:, both, 1], ALU.min)
-            nc.vector.tensor_tensor(high[:, both], high2[:, both, 0], high2[:, both, 1], ALU.max)
-            for r in range(2):
+            low = ring.tile([P, S], F32, name="low")
+            high = ring.tile([P, S], F32, name="high")
+            nc.vector.tensor_tensor(low[:, :count], low2[:, :count, 0], low2[:, :count, 1], ALU.min)
+            nc.vector.tensor_tensor(high[:, :count], high2[:, :count, 0], high2[:, :count, 1], ALU.max)
+            for r, t in enumerate(tiles):
                 part = slice(r * width, (r + 1) * width)
-                nc.vector.tensor_tensor(mb[:, part], h2_rows[2 * pair + r][:, lo:hi], low[:, part], ALU.subtract)
-            squashed = ring.tile([P, 2 * half], F32, name="squashed")
-            nc.scalar.activation(squashed[:, both], mb[:, both], ACT.Tanh)
-            return high[:, both], squashed[:, both]
+                nc.vector.tensor_tensor(mb[:, part], h2_rows[t][:, lo:hi], low[:, part], ALU.subtract)
+            squashed = ring.tile([P, S], F32, name="squashed")
+            nc.scalar.activation(squashed[:, :count], mb[:, :count], ACT.Tanh)
+            return high[:, :count], squashed[:, :count]
 
-        def finish(pair, lo, hi, high, squashed, last):
-            width = hi - lo
-            u, at = lo // half, lo % half
-            rows = slice(2 * pair, 2 * pair + 2)
+        def finish(tiles, lo, hi, high, squashed):
+            rows = slice(tiles[0], tiles[-1] + 1)
             nc.vector.tensor_tensor(
-                result[u][:, rows, at:at + width], high.rearrange("p (r j) -> p r j", r=2),
-                squashed.rearrange("p (r j) -> p r j", r=2), ALU.mult,
+                result[:, rows, lo:hi], high.rearrange("p (r j) -> p r j", r=len(tiles)),
+                squashed.rearrange("p (r j) -> p r j", r=len(tiles)), ALU.mult,
             )
-            nc.sync.dma_start(out_rows[:, rows, lo:hi], result[u][:, rows, at:at + width])
-            if pair == 1:
-                planes(lo, hi, last)
-                if hi % half == 0:
-                    store_scales(u)
+            nc.sync.dma_start(out_rows[:, rows, lo:hi], result[:, rows, lo:hi])
+            if tiles[-1] == PACK - 1:
+                planes(lo, hi)
 
-        def planes(lo, hi, last):
-            width = hi - lo
-            u, at = lo // half, lo % half
-            grouped = held("out_grouped%d" % lo, [P, width * PACK], BF16)
-            round_copy = nc.vector.tensor_copy if last else nc.scalar.copy
+        def planes(lo, hi):
+            grouped = held("out_grouped%d" % lo, [P, half * PACK], BF16)
+            round_copy = nc.vector.tensor_copy if hi == S else nc.scalar.copy
             round_copy(
                 grouped[:].rearrange("p (c i t) -> p c t i", i=4, t=PACK),
-                result[u][:, :, at:at + width].rearrange("p t (c i) -> p c t i", i=4),
+                result[:, :, lo:hi].rearrange("p t (c i) -> p c t i", i=4),
             )
-            codes = held("out_codes%d" % lo, [P, width], U32)
-            nc.vector.quantize_mx(out=codes[:].bitcast(FP8X4), scales=out_plane[u][:, at:at + width], in_=grouped[:])
+            codes = held("out_codes%d" % lo, [P, half], U32)
+            plane = held("out_plane%d" % lo, [P, half], U8)
+            nc.vector.quantize_mx(out=codes[:].bitcast(FP8X4), scales=plane[:], in_=grouped[:])
             nc.sync.dma_start(out_words[:, lo:hi], codes[:].bitcast(I32))
-
-        def store_scales(u):
             for j in range(4):
-                queue = nc.sync if j % 2 == 0 else nc.scalar
-                queue.dma_start(
-                    out_2[0, j:16:4, u * half:(u + 1) * half].bitcast(I32), out_plane[u][j:P:32, :].bitcast(I32)
-                )
+                queue = nc.sync if j == 0 else nc.scalar if j < 3 else nc.sync
+                queue.dma_start(out_2[0, j:16:4, lo:hi].bitcast(I32), plane[j:P:32, :].bitcast(I32))
 
-        quarter = half // 2
-        units = [(0, 0, half), (1, 0, half), (0, half, S), (1, half, half + quarter), (1, half + quarter, S)]
+        units = [((0,), 0, S), ((1,), 0, S), ((2, 3), 0, half), ((2,), half, S), ((3,), half, S)]
+        on_vector = (2, 0, 0, 0, 0)
         lag = 2
         made = []
         for n in range(len(units) + lag):
             if n < len(units):
-                made.append(members(*units[n], n == 0))
+                made.append(members(*units[n], on_vector[n]))
             if n >= lag:
-                finish(*units[n - lag], *made[n - lag], n - lag == len(units) - 1)
+                finish(*units[n - lag], *made[n - lag])

@@ -206,6 +206,7 @@ def tile_picked_pqlayfoldgtan_none_po_kernel(
         out_rows = out_0.rearrange("(p t) j -> p t j", t=PACK)
         out_words = out_1[0].rearrange("p n t -> p (n t)").bitcast(I32)
         result = held("result", [P, PACK, S], F32)
+        out_plane = held("out_plane", [P, S], U8)
 
         def members(tiles, lo, hi, on_vector):
             width = hi - lo
@@ -256,12 +257,8 @@ def tile_picked_pqlayfoldgtan_none_po_kernel(
                 result[:, :, lo:hi].rearrange("p t (c i) -> p c t i", i=4),
             )
             codes = held("out_codes%d" % lo, [P, half], U32)
-            plane = held("out_plane%d" % lo, [P, half], U8)
-            nc.vector.quantize_mx(out=codes[:].bitcast(FP8X4), scales=plane[:], in_=grouped[:])
+            nc.vector.quantize_mx(out=codes[:].bitcast(FP8X4), scales=out_plane[:, lo:hi], in_=grouped[:])
             nc.sync.dma_start(out_words[:, lo:hi], codes[:].bitcast(I32))
-            for j in range(4):
-                queue = nc.sync if j == 0 else nc.scalar if j < 3 else nc.sync
-                queue.dma_start(out_2[0, j:16:4, lo:hi].bitcast(I32), plane[j:P:32, :].bitcast(I32))
 
         units = [((0,), 0, S), ((1,), 0, S), ((2, 3), 0, half), ((2,), half, S), ((3,), half, S)]
         on_vector = (2, 0, 0, 0, 0)
@@ -272,3 +269,6 @@ def tile_picked_pqlayfoldgtan_none_po_kernel(
                 made.append(members(*units[n], on_vector[n]))
             if n >= lag:
                 finish(*units[n - lag], *made[n - lag])
+        for j in range(4):
+            queue = nc.sync if j == 0 else nc.scalar
+            queue.dma_start(out_2[0, j:16:4, :].bitcast(I32), out_plane[j:P:32, :].bitcast(I32))

@@ -19,8 +19,8 @@ ALU = mybir.AluOpType
 P = 128
 PACK = 4
 MEMBERS = 4
-SPARE = 8
-GATHER = 512
+SPARE = 520
+GATHER = 1024
 
 
 def tile_picked_pqlayfoldgtan_none_po_kernel(
@@ -51,7 +51,7 @@ def tile_picked_pqlayfoldgtan_none_po_kernel(
 
         d_scale_table = held("d_scale_table", [P, G], U8)
         x_scale_table = held("x_scale_table", [P, T], U8)
-        nc.vector.memset(x_scale_table[:].bitcast(I32), 0)
+        nc.gpsimd.memset(x_scale_table[:].bitcast(I32), 0)
         k1_list = load_list("k1_list", k1)
         load_scale_rows(nc.sync, d_scale_table, d_scales)
         offs_list = load_list("offs_list", offs)
@@ -106,7 +106,7 @@ def tile_picked_pqlayfoldgtan_none_po_kernel(
             )
 
         w_plane = keep.tile([P, N], U8, name="w_plane", tag="x_table", align_bytes=64)
-        nc.vector.tensor_copy(
+        nc.gpsimd.tensor_copy(
             w_plane[:].rearrange("p (t m) -> p t m", t=PACK),
             w_scale_rows[:].rearrange("p (m t) -> p t m", t=PACK),
         )
@@ -223,7 +223,7 @@ def tile_picked_pqlayfoldgtan_none_po_kernel(
             quads = mb[:, :count * MEMBERS].rearrange("p (j a e) -> p j a e", a=2, e=2)
             low2 = ring.tile([P, S, 2], F32, name="low2")
             high2 = ring.tile([P, S, 2], F32, name="high2")
-            step = count if on_vector == 2 else half
+            step = count if on_vector else half
             for at in range(0, count, step):
                 part = slice(at, at + step)
                 nc.vector.tensor_tensor(low2[:, part, :], quads[:, part, 0, :], quads[:, part, 1, :], ALU.min)
@@ -261,7 +261,7 @@ def tile_picked_pqlayfoldgtan_none_po_kernel(
             nc.sync.dma_start(out_words[:, lo:hi], codes[:].bitcast(I32))
 
         units = [((0,), 0, S), ((1,), 0, S), ((2, 3), 0, half), ((2,), half, S), ((3,), half, S)]
-        on_vector = (2, 0, 0, 0, 0)
+        on_vector = (1, 0, 0, 0, 0)
         lag = 2
         made = []
         for n in range(len(units) + lag):

from contextlib import ExitStack

import concourse.mybir as mybir

K, T, S, N, G, H, W = 512, 2048, 512, 512, 2048, 512, 256
FLOPS = 2 * K * H * S + 2 * H * N * S

F32 = mybir.dt.float32
BF16 = mybir.dt.bfloat16
I32 = mybir.dt.int32
U32 = mybir.dt.uint32
U16 = mybir.dt.uint16
U8 = mybir.dt.uint8
FP8X4 = mybir.dt.float8_e4m3fn_x4
FP4X4 = mybir.dt.float4_e2m1fn_x4
ACT = mybir.ActivationFunctionType
ALU = mybir.AluOpType

P = 128
PACK = 4
MEMBERS = 4
SPARE = 520
GATHER = 1024


def tile_picked_pqlayfoldgtan_none_po_kernel(
    tc, x_words, x_scales, d_words, d_scales, gn, w1_words, w1_scales, offs, k1, n1, n2, n3, out_0, out_1, out_2
):
    nc = tc.nc
    with ExitStack() as ctx:
        lists = ctx.enter_context(tc.tile_pool(name="lists", bufs=1))
        keep = ctx.enter_context(tc.tile_pool(name="keep", bufs=1))
        ring = ctx.enter_context(tc.tile_pool(name="ring", bufs=3))
        psum = ctx.enter_context(tc.psum_pool(name="psum", bufs=1))

        def held(name, shape, dtype):
            return keep.tile(shape, dtype, name=name, align_bytes=64)

        def load_list(name, src):
            tile = lists.tile(list(src.shape), U16, name=name)
            nc.sync.dma_start(tile[:], src)
            return tile

        def shared(name, shape, dtype, tag):
            return keep.tile(shape, dtype, name=name, tag=tag, align_bytes=64)

        def load_scale_rows(queue, table, scales):
            width = scales.shape[2]
            rows = scales[0].bitcast(I32).unsqueeze(1).to_broadcast([16, 8, width // 4])
            queue.dma_start(table[:].bitcast(I32), rows)

        d_scale_table = held("d_scale_table", [P, G], U8)
        x_scale_table = held("x_scale_table", [P, T], U8)
        nc.gpsimd.memset(x_scale_table[:].bitcast(I32), 0)
        k1_list = load_list("k1_list", k1)
        load_scale_rows(nc.sync, d_scale_table, d_scales)
        offs_list = load_list("offs_list", offs)
        n2_list = load_list("n2_list", n2)
        n1_list = load_list("n1_list", n1)
        n3_list = load_list("n3_list", n3)
        nc.sync.dma_start(x_scale_table[0:P:8, :].bitcast(I32), x_scales[0].bitcast(I32))
        d_table = shared("d_table", [P, G], U32, "d_table")
        nc.sync.dma_start(d_table[:].bitcast(I32), d_words[0].rearrange("p n t -> p (n t)").bitcast(I32))
        x_table = shared("x_table", [P, T], U32, "x_table")
        nc.sync.dma_start(x_table[:].bitcast(I32), x_words[0].rearrange("p n t -> p (n t)").bitcast(I32))
        h2_rows = [held("h2_%d" % t, [P, S + SPARE], F32) for t in range(PACK)]
        for t in range(PACK):
            nc.gpsimd.memset(h2_rows[t][:, S:], 0.0)

        def gather_scale_rows(queue, plane):
            for j in range(1, 4):
                queue.dma_start(plane[j:P:32, :].bitcast(I32), plane[8 * j:P:32, :].bitcast(I32))

        d_scale_picked = held("d_scale_picked", [P, H], U8)
        nc.vector.tensor_copy(d_scale_picked[:], d_scale_table[:].indirect(k1_list[:]))
        d_plane = held("d_plane", [P, H], U8)
        nc.vector.tensor_copy(
            d_plane[:].rearrange("p (t m) -> p t m", t=PACK),
            d_scale_picked[:].rearrange("p (m t) -> p t m", t=PACK),
        )
        gather_scale_rows(nc.scalar, d_plane)
        x_scale_picked = shared("x_scale_picked", [P, S], U8, "x_scale_picked")
        nc.vector.tensor_copy(x_scale_picked[:], x_scale_table[:].indirect(offs_list[:]))
        x_plane = held("x_plane", [P, S], U8)
        nc.vector.tensor_copy(x_plane[:].bitcast(I32), x_scale_picked[:].bitcast(I32))
        gather_scale_rows(nc.scalar, x_plane)
        w_scale_rows = shared("w_scale_rows", [P, N], U8, "x_scale_picked")
        load_scale_rows(nc.scalar, w_scale_rows, w1_scales)
        d_picked = shared("d_picked", [P, H], U32, "d_picked")
        nc.vector.tensor_copy(d_picked[:], d_table[:].indirect(k1_list[:]))
        w_raw = shared("w_raw", [P, 2 * N], U8, "d_table")
        nc.sync.dma_start(w_raw[:].bitcast(I32), w1_words[0].bitcast(I32))
        d_codes = held("d_codes", [P, H], U32)
        nc.vector.tensor_copy(
            d_codes[:].rearrange("p (t m) -> p m t", t=PACK),
            d_picked[:].rearrange("p (m t) -> p m t", t=PACK),
        )
        gain = shared("gain", [P, PACK], F32, "d_picked")
        nc.sync.dma_start(gain[:], gn.rearrange("(p t) o -> p (t o)", t=PACK))
        x_codes = held("x_codes", [P, S], U32)
        half = S // 2
        for u in range(2):
            nc.vector.tensor_copy(
                x_codes[:, u * half:(u + 1) * half],
                x_table[:].indirect(offs_list[:, u * half // 16:(u + 1) * half // 16]),
            )

        w_plane = keep.tile([P, N], U8, name="w_plane", tag="x_table", align_bytes=64)
        nc.gpsimd.tensor_copy(
            w_plane[:].rearrange("p (t m) -> p t m", t=PACK),
            w_scale_rows[:].rearrange("p (m t) -> p t m", t=PACK),
        )
        gather_scale_rows(nc.sync, w_plane)

        z_pairs = held("z_pairs", [P, 2, S, 2], BF16)

        def accumulators(name):
            acc = []
            for t in range(PACK):
                if t < 2:
                    acc.append([psum.tile([P, half], F32, name="%s%d_%d" % (name, t, u), tag="bank%d_%d" % (t, u))[:] for u in range(2)])
                else:
                    bank = psum.tile([P, S], F32, name="%s%d" % (name, t), tag="bank%d" % t)
                    acc.append([bank[:, :half], bank[:, half:], bank[:]])
            return acc

        def pieces(acc, t):
            if t < 2:
                return [(slice(u * half, (u + 1) * half), acc[t][u]) for u in range(2)]
            return [(slice(0, S), acc[t][2])]

        h_acc = accumulators("h_acc")
        pass_order = [(t, u) for pair in range(2) for u in range(2) for t in (2 * pair, 2 * pair + 1)]
        for t, u in pass_order:
            tokens = slice(u * half, (u + 1) * half)
            cols = slice(t * P, (t + 1) * P)
            nc.tensor.matmul_mx(
                out=h_acc[t][u], lhsT=d_codes[:, cols].bitcast(FP8X4), lhsT_scale=d_plane[:, cols],
                rhs=x_codes[:, tokens].bitcast(FP8X4), rhs_scale=x_plane[:, tokens], start=True, stop=True,
            )
        h_rows = [held("h%d" % t, [P, S], F32) for t in range(PACK)]
        for t in range(PACK):
            for cols, acc in pieces(h_acc, t):
                nc.vector.tensor_scalar(h_rows[t][:, cols], acc, 0.0625, None, ALU.mult)
        gate = [held("gate%d" % t, [P, W], F32) for t in range(PACK)]
        fetched = [keep.tile([P, W], F32, name="fetched%d" % t, tag="fetched%d" % t, align_bytes=64) for t in range(PACK)]

        def fetch_gate(t):
            nc.scalar.activation(gate[t][:], h_rows[t][:].indirect(n2_list[:]), ACT.Sigmoid)

        def fetch_partner(t):
            nc.scalar.activation(fetched[t][:], h_rows[t][:].indirect(n1_list[:]), ACT.Copy)

        fetch_gate(0)
        fetch_gate(1)
        fetch_partner(0)
        fetch_gate(2)
        fetch_gate(3)
        fetch_partner(3)
        for t in (1, 0, 2, 3):
            if t in (0, PACK - 1):
                nc.vector.tensor_tensor(h_rows[t][:].indirect(n2_list[:]), fetched[t][:], gate[t][:], ALU.mult)
            else:
                nc.vector.tensor_tensor(fetched[t][:], h_rows[t][:].indirect(n1_list[:]), gate[t][:], ALU.mult)
                nc.scalar.activation(h_rows[t][:].indirect(n2_list[:]), fetched[t][:], ACT.Copy)

        def round_gained(t, cols):
            nc.vector.tensor_scalar(z_pairs[:, t // 2, cols, t % 2], h_rows[t][:, cols], gain[:, t:t + 1], None, ALU.mult)

        for t in (0, 3, 1):
            round_gained(t, slice(0, S))
        w_codes = keep.tile([P, 2 * N], U8, name="w_codes", tag="fetched2", align_bytes=64)
        nc.scalar.copy(
            w_codes[:].bitcast(U16).rearrange("p (t m) -> p t m", t=PACK),
            w_raw[:].bitcast(U16).rearrange("p (m t) -> p t m", t=PACK),
        )

        z_codes = held("z_codes", [P, S], U32)
        z_plane = held("z_plane", [P, S], U8)
        z_words = z_pairs[:].rearrange("p a j e -> p a (j e)").bitcast(I32)
        h2_acc = accumulators("h2_acc")
        z_grouped = [held("z_grouped%d" % u, [P, half * PACK], BF16) for u in range(2)]
        for u in range(2):
            cols = slice(u * half, (u + 1) * half)
            round_gained(2, cols)
            nc.vector.tensor_copy(
                z_grouped[u][:].bitcast(I32).rearrange("p (j a) -> p j a", a=2),
                z_words[:, :, cols].rearrange("p a j -> p j a"),
            )
        for u in range(2):
            cols = slice(u * half, (u + 1) * half)
            nc.vector.quantize_mx(out=z_codes[:, cols].bitcast(FP8X4), scales=z_plane[:, cols], in_=z_grouped[u][:])
        for t, u in pass_order:
            cols = slice(u * half, (u + 1) * half)
            nc.tensor.matmul_mx(
                out=h2_acc[t][u],
                lhsT=w_codes[:, 2 * t * P:2 * (t + 1) * P].bitcast(FP4X4),
                lhsT_scale=w_plane[:, t * P:(t + 1) * P],
                rhs=z_codes[:, cols].bitcast(FP8X4), rhs_scale=z_plane[:, cols], start=True, stop=True,
            )
        for t in range(PACK):
            empty = nc.vector.tensor_copy if t % 2 == 1 else nc.scalar.copy
            for cols, acc in pieces(h2_acc, t):
                empty(h2_rows[t][:, cols], acc)

        out_rows = out_0.rearrange("(p t) j -> p t j", t=PACK)
        out_words = out_1[0].rearrange("p n t -> p (n t)").bitcast(I32)
        result = held("result", [P, PACK, S], F32)
        out_plane = held("out_plane", [P, S], U8)

        def members(tiles, lo, hi, on_vector):
            width = hi - lo
            count = len(tiles) * width
            mb = ring.tile([P, S * MEMBERS], F32, name="mb")
            looks = [(t, e) for t in tiles for e in range(lo * MEMBERS, hi * MEMBERS, GATHER)]
            for n, (t, e) in enumerate(looks):
                window = h2_rows[t][:].indirect(n3_list[:, e // 16:(e + GATHER) // 16])
                dst = mb[:, n * GATHER:(n + 1) * GATHER]
                if n >= len(looks) - on_vector:
                    nc.vector.tensor_copy(dst, window)
                else:
                    nc.scalar.activation(dst, window, ACT.Copy)
            quads = mb[:, :count * MEMBERS].rearrange("p (j a e) -> p j a e", a=2, e=2)
            low2 = ring.tile([P, S, 2], F32, name="low2")
            high2 = ring.tile([P, S, 2], F32, name="high2")
            step = count if on_vector else half
            for at in range(0, count, step):
                part = slice(at, at + step)
                nc.vector.tensor_tensor(low2[:, part, :], quads[:, part, 0, :], quads[:, part, 1, :], ALU.min)
                nc.vector.tensor_tensor(high2[:, part, :], quads[:, part, 0, :], quads[:, part, 1, :], ALU.max)
            low = ring.tile([P, S], F32, name="low")
            high = ring.tile([P, S], F32, name="high")
            nc.vector.tensor_tensor(low[:, :count], low2[:, :count, 0], low2[:, :count, 1], ALU.min)
            nc.vector.tensor_tensor(high[:, :count], high2[:, :count, 0], high2[:, :count, 1], ALU.max)
            for r, t in enumerate(tiles):
                part = slice(r * width, (r + 1) * width)
                nc.vector.tensor_tensor(mb[:, part], h2_rows[t][:, lo:hi], low[:, part], ALU.subtract)
            squashed = ring.tile([P, S], F32, name="squashed")
            nc.scalar.activation(squashed[:, :count], mb[:, :count], ACT.Tanh)
            return high[:, :count], squashed[:, :count]

        def finish(tiles, lo, hi, high, squashed):
            rows = slice(tiles[0], tiles[-1] + 1)
            nc.vector.tensor_tensor(
                result[:, rows, lo:hi], high.rearrange("p (r j) -> p r j", r=len(tiles)),
                squashed.rearrange("p (r j) -> p r j", r=len(tiles)), ALU.mult,
            )
            nc.sync.dma_start(out_rows[:, rows, lo:hi], result[:, rows, lo:hi])
            if tiles[-1] == PACK - 1:
                planes(lo, hi)

        def planes(lo, hi):
            grouped = held("out_grouped%d" % lo, [P, half * PACK], BF16)
            round_copy = nc.vector.tensor_copy if hi == S else nc.scalar.copy
            round_copy(
                grouped[:].rearrange("p (c i t) -> p c t i", i=4, t=PACK),
                result[:, :, lo:hi].rearrange("p t (c i) -> p c t i", i=4),
            )
            codes = held("out_codes%d" % lo, [P, half], U32)
            nc.vector.quantize_mx(out=codes[:].bitcast(FP8X4), scales=out_plane[:, lo:hi], in_=grouped[:])
            nc.sync.dma_start(out_words[:, lo:hi], codes[:].bitcast(I32))

        units = [((0,), 0, S), ((1,), 0, S), ((2, 3), 0, half), ((2,), half, S), ((3,), half, S)]
        on_vector = (1, 0, 0, 0, 0)
        lag = 2
        made = []
        for n in range(len(units) + lag):
            if n < len(units):
                made.append(members(*units[n], on_vector[n]))
            if n >= lag:
                finish(*units[n - lag], *made[n - lag])
        for j in range(4):
            queue = nc.sync if j == 0 else nc.scalar
            queue.dma_start(out_2[0, j:16:4, :].bitcast(I32), out_plane[j:P:32, :].bitcast(I32))
